import numpy as np
import ml_dtypes


def mxq(x, axis, fmt="e4m3"):
    dtype, down = {"e4m3": (ml_dtypes.float8_e4m3fn, 7), "e5m2": (ml_dtypes.float8_e5m2, 14)}[fmt]
    v = np.moveaxis(np.asarray(x, np.float32).astype(ml_dtypes.bfloat16).astype(np.float64), axis, -1)
    blocks = v.reshape(v.shape[:-1] + (-1, 32))
    amax = np.abs(blocks).max(-1, keepdims=True)
    byte = np.maximum(np.where(amax > 0, np.frexp(amax)[1] - 1 + 127, 0) - down, 1)
    scale = np.exp2(byte - 127.0)
    codes = (blocks / scale).astype(np.float32).astype(dtype).astype(np.float64)
    return np.moveaxis((codes * scale).reshape(v.shape), -1, axis)


WIDE = False


def mx_kscale(k):
    if not WIDE:
        return np.ones(k)
    levels = np.array([10, -10, 5, -5, 0])
    if k % 512:
        return np.exp2(np.random.permutation(np.resize(levels, k // 32))).repeat(32)
    a = np.empty((k // 512, 16))
    for p in range(k // 512):
        a[p, :8] = np.random.permutation(np.resize(levels, 8))
        for g in range(8):
            far = levels[np.abs(levels - a[p, g]) >= 10]
            a[p, g + 8] = far[np.random.randint(len(far))]
    return np.exp2(a.ravel()).repeat(32)


def f64(x):
    return np.asarray(x).astype(np.float64)


def striped(idx):
    return np.tile(np.asarray(idx).reshape(-1, 16).T, (8, 1)).astype(np.uint16)


def unstriped(offs):
    return offs[:16].T.reshape(-1).astype(np.int64)


E2M1 = np.array([0.0, 0.5, 1.0, 1.5, 2.0, 3.0, 4.0, 6.0, -0.0, -0.5, -1.0, -1.5, -2.0, -3.0, -4.0, -6.0])


def pack_weight(w, fmt):
    k, n = w.shape
    w = f64(np.asarray(w, np.float32).astype(ml_dtypes.bfloat16)).reshape(k // 32, 32, n)
    amax = np.abs(w).max(1)
    if fmt == "e4m3":
        byte = np.frexp(amax)[1] - 1 + 127 - 7
    else:
        mant, ex = np.frexp(amax / 6.0)
        byte = np.where(mant > 0.5, ex, ex - 1) + 127
    byte = np.clip(np.where(amax > 0, byte, 1), 1, 254)
    scaled = (w * np.exp2(127.0 - byte)[:, None, :]).reshape(k, n).astype(np.float32)
    by_word = np.ascontiguousarray(scaled.reshape(k // 512, 128, 4, n).transpose(0, 1, 3, 2))
    if fmt == "e4m3":
        words = by_word.astype(ml_dtypes.float8_e4m3fn).view(np.uint8)
    else:
        c = by_word.astype(ml_dtypes.float4_e2m1fn).view(np.uint8) & 0xF
        words = (c[..., 0::2] | (c[..., 1::2] << 4)).reshape(k // 512, 128, 2 * n)
    return np.ascontiguousarray(words), np.ascontiguousarray(byte.astype(np.uint8).reshape(k // 512, 16, n))


def unpack_weight(words, scales, fmt):
    g, _, n = scales.shape
    words = np.ascontiguousarray(words).reshape(g, 128, n, -1)
    if fmt == "e4m3":
        vals = words.view(ml_dtypes.float8_e4m3fn).astype(np.float64)
    else:
        nib = np.empty((g, 128, n, 4), np.uint8)
        nib[..., 0::2] = words & 0xF
        nib[..., 1::2] = words >> 4
        vals = E2M1[nib]
    vals = vals * np.repeat(np.exp2(scales.astype(np.float64) - 127.0), 8, axis=1)[..., None]
    return vals.transpose(0, 1, 3, 2).reshape(g * 512, n)


D, E, T, I, Q = 512, 512, 2048, 512, 128


def setup_inputs():
    n = np.random.standard_normal
    idx = np.random.permutation(T)[:I]
    fd = mx_kscale(D)
    fe = mx_kscale(E)
    fi = mx_kscale(I)
    ti = np.ones(T)
    ti[idx] = fi
    keysp = pack_weight(n((D, T)) / fd[:, None], "e2m1")
    valsp = pack_weight(n((E, T)) / fe[:, None], "e2m1")
    return {
        "query": (n((D, Q)) * 0.6 / np.sqrt(D) * fd[:, None]).astype(np.float32),
        "keys_words": keysp[0],
        "keys_scales": keysp[1],
        "age": np.tile(np.random.uniform(0.0, 2.0, T), (128, 1)).astype(np.float32),
        "rate": (np.random.uniform(0.3, 1.2, (Q, 1))).astype(np.float32),
        "reserve": (np.random.uniform(20.0, 100.0, (Q, 1))).astype(np.float32),
        "gout": (n((E, Q)) * 1 / np.sqrt(E) * fe[:, None]).astype(np.float32),
        "vals_words": valsp[0],
        "vals_scales": valsp[1],
        "size": (np.random.uniform(0.5, 2.0, (1, I))).astype(np.float32),
        "fs": (np.random.uniform(128.0, 512.0, (1, I)) * fi).astype(np.float32),
        "keyrows": (n((D, T)) / ti).astype(np.float32),
        "res": (n((Q, D)) * 4.0).astype(np.float32),
        "offs": striped(idx),
    }


def reference(query, keys_words, keys_scales, age, rate, reserve, gout, vals_words, vals_scales, size, fs, keyrows, res, offs):
    idx = unstriped(offs)
    keysu = unpack_weight(keys_words, keys_scales, "e2m1")
    valsu = unpack_weight(vals_words, vals_scales, "e2m1")
    queryq = mxq(f64(query), 0, "e4m3")
    keysidxg = keysu[:, idx]
    a = queryq.T @ keysidxg
    p = np.exp(a - f64(age)[:1][:, idx] * f64(rate))
    z = np.sum(p, axis=1, keepdims=True) + f64(reserve)
    goutq = mxq(f64(gout), 0, "e4m3")
    valsidxg = valsu[:, idx]
    c0 = goutq.T @ valsidxg
    dz = np.sum(c0 * p * f64(size) / np.square(z) * (-1.0), axis=1, keepdims=True)
    dp = c0 / z * f64(size) + dz
    da = dp * p
    gs = da * f64(fs)
    gt1 = gs.T
    kt = f64(keyrows)[:, idx].T
    gt1q = mxq(gt1, 0, "e4m3")
    ktq = mxq(kt, 0, "e4m3")
    gq = gt1q.T @ ktq
    y = gq + f64(res)
    return y

@@ -1,0 +1,176 @@
+from contextlib import ExitStack
+
+import concourse.mybir as mybir
+from concourse.masks import make_identity
+
+D, E, T, I, Q = 512, 512, 2048, 512, 128
+FLOPS = 2 * Q * I * (D + E + D)
+P = 128
+PACK = 4
+F32 = mybir.dt.float32
+BF16 = mybir.dt.bfloat16
+I32 = mybir.dt.int32
+U32 = mybir.dt.uint32
+U16 = mybir.dt.uint16
+U8 = mybir.dt.uint8
+FP8X4 = mybir.dt.float8_e4m3fn_x4
+FP4X4 = mybir.dt.float4_e2m1fn_x4
+ALU = mybir.AluOpType
+ACT = mybir.ActivationFunctionType
+
+
+def tile_attend_bfadereserve_q_kernel(tc, query, keys_words, keys_scales, age, rate, reserve, gout,
+                                       vals_words, vals_scales, size, fs, keyrows, res, offs, out):
+    nc = tc.nc
+    with ExitStack() as ctx:
+        sb = ctx.enter_context(tc.tile_pool(name="sb", bufs=1))
+        ps = ctx.enter_context(tc.psum_pool(name="ps", bufs=1))
+        turn = ctx.enter_context(tc.psum_pool(name="turn", bufs=3))
+
+        offsets = sb.tile([P, I // 16], U16, name="offsets")
+        kw = sb.tile([P, T], U16, name="kw", align_bytes=64)
+        vw = sb.tile([P, T], U16, name="vw", align_bytes=64)
+        ks = sb.tile([P, T], U8, name="ks", align_bytes=64)
+        vs = sb.tile([P, T], U8, name="vs", align_bytes=64)
+        age_win = sb.tile([P, T], F32, name="age_win", align_bytes=64)
+        q_raw = sb.tile([P, PACK, Q], F32, name="q_raw")
+        g_raw = sb.tile([P, PACK, Q], F32, name="g_raw")
+        kr0 = [sb.tile([P, T // 2], F32, name="kr0_%d" % h, align_bytes=64) for h in range(2)]
+        kr = [sb.tile([P, T], F32, name="kr%d" % j, align_bytes=64) for j in range(1, 4)]
+        res_sb = sb.tile([P, D], F32, name="res_sb")
+        rate_sb = sb.tile([P, 1], F32, name="rate_sb")
+        reserve_sb = sb.tile([P, 1], F32, name="reserve_sb")
+        size_c = sb.tile([P, PACK], F32, name="size_c")
+        fs_c = sb.tile([P, PACK], F32, name="fs_c")
+        ident = sb.tile([P, P], F32, name="ident")
+        warm = sb.tile([P, 1], F32, name="warm")
+
+        nc.vector.memset(ks[:].bitcast(I32), 0)
+        nc.vector.memset(age_win[:], 0.0)
+        nc.vector.memset(vs[:].bitcast(I32), 0)
+        make_identity(nc, ident[:])
+        nc.scalar.activation(warm[:], ident[:, 0:1], ACT.Exp)
+
+        def load_scales(dst, src):
+            for b in range(4):
+                nc.sync.dma_start(dst[32 * b:32 * b + 4, :].bitcast(I32), src[0, 4 * b:4 * b + 4, :].bitcast(I32))
+
+        def load_column(dst, src):
+            with nc.allow_non_contiguous_dma(reason="one value a partition"):
+                nc.sync.dma_start(dst[:], src)
+
+        nc.sync.dma_start(offsets[:], offs)
+        nc.sync.dma_start(kw[:].bitcast(I32), keys_words[0].bitcast(I32))
+        nc.sync.dma_start(q_raw[:], query.rearrange("(p j) w -> p j w", j=PACK))
+        load_scales(ks, keys_scales)
+        nc.sync.dma_start(vw[:].bitcast(I32), vals_words[0].bitcast(I32))
+        nc.sync.dma_start(g_raw[:], gout.rearrange("(p j) w -> p j w", j=PACK))
+        nc.sync.dma_start(age_win[0:1, :], age[0:1, :])
+        load_column(rate_sb, rate)
+        nc.sync.dma_start(kr0[0][:], keyrows[0:P, 0:T // 2])
+        load_scales(vs, vals_scales)
+        nc.sync.dma_start(kr0[1][:], keyrows[0:P, T // 2:T])
+        load_column(size_c, size.rearrange("o (p j) -> p (o j)", j=PACK))
+        load_column(reserve_sb, reserve)
+        load_column(fs_c, fs.rearrange("o (p j) -> p (o j)", j=PACK))
+        for j in range(1, 4):
+            nc.sync.dma_start(kr[j - 1][:], keyrows[j * P:(j + 1) * P, :])
+        nc.sync.dma_start(res_sb[:], res)
+
+        def quantize(name, grouped):
+            codes = sb.tile([P, P], U32, name=name + "_codes", align_bytes=64)
+            scales = sb.tile([P, P], U8, name=name + "_scales", align_bytes=64)
+            nc.vector.quantize_mx(out=codes[:].bitcast(FP8X4), scales=scales[:], in_=grouped[:])
+            return codes, scales
+
+        def interleave(name, raw):
+            grouped = sb.tile([P, Q * PACK], BF16, name=name + "_grp", align_bytes=64)
+            nc.scalar.copy(grouped[:].rearrange("p (w j) -> p w j", j=PACK), raw[:].rearrange("p j w -> p w j"))
+            return grouped
+
+        def gather(name, window, dtype):
+            got = sb.tile([P, I], dtype, name=name, align_bytes=64)
+            nc.vector.tensor_copy(got[:], window[:].indirect(offsets[:]))
+            return got
+
+        def turn_pairs(name, rows):
+            words = rows[:].bitcast(F32)
+            bank = turn.tile([P, 2, P], F32, name="turn")
+            for u in range(2):
+                nc.tensor.transpose(bank[:, u, :], words[:, u:2 * P:2], ident[:])
+            grouped = sb.tile([P, P * PACK], BF16, name=name + "_grp", align_bytes=64)
+            nc.scalar.copy(grouped[:].bitcast(F32).rearrange("p (r u) -> p r u", u=2), bank[:].rearrange("p u r -> p r u"))
+            return grouped
+
+        def spread(name, cols):
+            bank = ps.tile([P, PACK, P], F32, name=name)
+            for j in range(PACK):
+                nc.tensor.transpose(bank[:, j, :], cols[:, j:j + 1].to_broadcast([P, P]), ident[:])
+            return bank
+
+        kw_g = gather("kw_g", kw, U16)
+        q_grp = interleave("q", q_raw)
+        ks_g = gather("ks_g", ks, U8)
+        q_codes, q_scales = quantize("q", q_grp)
+        a_ps = ps.tile([P, I], F32, name="bank_a")
+        nc.tensor.matmul_mx(out=a_ps[:], lhsT=q_codes[:].bitcast(FP8X4), lhsT_scale=q_scales[:],
+                            rhs=kw_g[:].bitcast(FP4X4), rhs_scale=ks_g[:], start=True, stop=True)
+        age_g = gather("age_g", age_win, F32)
+        age_t = turn.tile([P, PACK, P], F32, name="turn")
+        for j in range(PACK):
+            nc.tensor.transpose(age_t[:, j, :], age_g[:, j * P:(j + 1) * P], ident[:])
+        age_c = sb.tile([P, PACK], F32, name="age_c")
+        nc.scalar.copy(age_c[:], age_t[:, :, 0])
+        age_bc = spread("age_bc", age_c)
+        fade = sb.tile([P, I], F32, name="fade")
+        nc.scalar.activation(fade[:], age_bc[:].rearrange("p j s -> p (j s)"), ACT.Copy, scale=rate_sb[:])
+        vw_g = gather("vw_g", vw, U16)
+        g_grp = interleave("go", g_raw)
+        vs_g = gather("vs_g", vs, U8)
+        go_codes, go_scales = quantize("go", g_grp)
+        c_ps = ps.tile([P, I], F32, name="bank_c")
+        nc.tensor.matmul_mx(out=c_ps[:], lhsT=go_codes[:].bitcast(FP8X4), lhsT_scale=go_scales[:],
+                            rhs=vw_g[:].bitcast(FP4X4), rhs_scale=vs_g[:], start=True, stop=True)
+        size_bc = spread("size_bc", size_c)
+        size_sb = sb.tile([P, I], F32, name="size_sb")
+        nc.scalar.copy(size_sb[:].rearrange("p (s j) -> p s j", j=PACK), size_bc[:].rearrange("p j s -> p s j"))
+        fs_bc = spread("fs_bc", fs_c)
+
+        s_sb = sb.tile([P, I], F32, name="s_sb")
+        nc.vector.tensor_tensor(s_sb[:], a_ps[:], fade[:], ALU.subtract)
+        p_sb = sb.tile([P, I], F32, name="p_sb")
+        z0 = sb.tile([P, 1], F32, name="z0")
+        nc.scalar.activation(p_sb[:], s_sb[:], ACT.Exp, accum_out=z0[:])
+        u_sb = sb.tile([P, I], F32, name="u_sb")
+        nc.vector.tensor_tensor(u_sb[:], c_ps[:], size_sb[:], ALU.mult)
+        z = sb.tile([P, 1], F32, name="z")
+        nc.vector.tensor_tensor(z[:], z0[:], reserve_sb[:], ALU.add)
+        rz = sb.tile([P, 1], F32, name="rz")
+        nc.vector.reciprocal(rz[:], z[:])
+        t_sb = sb.tile([P, I], F32, name="t_sb")
+        r1 = sb.tile([P, 1], F32, name="r1")
+        nc.vector.scalar_tensor_tensor(t_sb[:], u_sb[:], rz[:], p_sb[:], ALU.mult, ALU.mult, accum_out=r1[:])
+        w_sb = sb.tile([P, I], F32, name="w_sb")
+        nc.vector.scalar_tensor_tensor(w_sb[:].rearrange("p (s j) -> p s j", j=PACK),
+                                       p_sb[:].rearrange("p (s j) -> p s j", j=PACK), rz[:],
+                                       fs_bc[:].rearrange("p j s -> p s j"), ALU.mult, ALU.mult)
+        gs = sb.tile([P, I], BF16, name="gs", align_bytes=64)
+        nc.vector.scalar_tensor_tensor(gs[:], u_sb[:], r1[:], w_sb[:], ALU.subtract, ALU.mult)
+        gs_codes, gs_scales = quantize("gs", turn_pairs("gs", gs))
+
+        kr0_bf = sb.tile([P, T], BF16, name="kr0_bf", align_bytes=64)
+        for c in range(4):
+            nc.scalar.activation(kr0_bf[:, c * 512:(c + 1) * 512], kr0[c // 2][:, (c % 2) * 512:(c % 2 + 1) * 512], ACT.Copy)
+        kt0 = sb.tile([P, I], BF16, name="kt0", align_bytes=64)
+        nc.scalar.activation(kt0[:], kr0_bf[:].indirect(offsets[:]), ACT.Copy)
+        o_ps = [ps.tile([P, 3 * P], F32, name="bank_a"), ps.tile([P, P], F32, name="bank_c")]
+        for j in range(4):
+            rows = kt0 if j == 0 else gather("kt%d" % j, kr[j - 1], BF16)
+            codes, scales = quantize("kt%d" % j, turn_pairs("kt%d" % j, rows))
+            dst = o_ps[0][:, j * P:(j + 1) * P] if j < 3 else o_ps[1][:]
+            nc.tensor.matmul_mx(out=dst, lhsT=gs_codes[:].bitcast(FP8X4), lhsT_scale=gs_scales[:],
+                                rhs=codes[:].bitcast(FP8X4), rhs_scale=scales[:], start=True, stop=True)
+        for k, (lo, hi) in enumerate(((0, 3 * P), (3 * P, D))):
+            y = sb.tile([P, hi - lo], F32, name="y%d" % k)
+            nc.vector.tensor_tensor(y[:], o_ps[k][:], res_sb[:, lo:hi], ALU.add)
+            nc.sync.dma_start(out[:, lo:hi], y[:])

@@ -5,8 +5,15 @@ from concourse.masks import make_identity
 
 D, E, T, I, Q = 512, 512, 2048, 512, 128
 FLOPS = 2 * Q * I * (D + E + D)
+
 P = 128
 PACK = 4
+BANK = 512
+BLOCKS = D // P
+LAST = BLOCKS - 1
+TURN_BANKS = 4
+SIZE_AT, FS_AT, RATE_AT, RESERVE_AT, SMALL_ROWS = 0, 4, 8, 9, 10
+
 F32 = mybir.dt.float32
 BF16 = mybir.dt.bfloat16
 I32 = mybir.dt.int32
@@ -24,153 +31,177 @@ def tile_attend_bfadereserve_q_kernel(tc, query, keys_words, keys_scales, age, r
     nc = tc.nc
     with ExitStack() as ctx:
         sb = ctx.enter_context(tc.tile_pool(name="sb", bufs=1))
-        ps = ctx.enter_context(tc.psum_pool(name="ps", bufs=1))
-        turn = ctx.enter_context(tc.psum_pool(name="turn", bufs=3))
+        held = ctx.enter_context(tc.psum_pool(name="held", bufs=1))
+        turn = ctx.enter_context(tc.psum_pool(name="turn", bufs=TURN_BANKS))
 
         offsets = sb.tile([P, I // 16], U16, name="offsets")
-        kw = sb.tile([P, T], U16, name="kw", align_bytes=64)
-        vw = sb.tile([P, T], U16, name="vw", align_bytes=64)
-        ks = sb.tile([P, T], U8, name="ks", align_bytes=64)
-        vs = sb.tile([P, T], U8, name="vs", align_bytes=64)
+        keys_w = sb.tile([P, T], U16, name="keys_w", tag="keys_w", align_bytes=64)
+        vals_w = sb.tile([P, T], U16, name="vals_w", tag="vals_w", align_bytes=64)
+        keys_s = sb.tile([P, T], U8, name="keys_s", align_bytes=64)
+        vals_s = sb.tile([P, T], U8, name="vals_s", align_bytes=64)
         age_win = sb.tile([P, T], F32, name="age_win", align_bytes=64)
-        q_raw = sb.tile([P, PACK, Q], F32, name="q_raw")
-        g_raw = sb.tile([P, PACK, Q], F32, name="g_raw")
-        kr0 = [sb.tile([P, T // 2], F32, name="kr0_%d" % h, align_bytes=64) for h in range(2)]
-        kr = [sb.tile([P, T], F32, name="kr%d" % j, align_bytes=64) for j in range(1, 4)]
-        res_sb = sb.tile([P, D], F32, name="res_sb")
-        rate_sb = sb.tile([P, 1], F32, name="rate_sb")
-        reserve_sb = sb.tile([P, 1], F32, name="reserve_sb")
-        size_c = sb.tile([P, PACK], F32, name="size_c")
-        fs_c = sb.tile([P, PACK], F32, name="fs_c")
+        age_cols = sb.tile([P, T // P], F32, name="age_cols", tag="age_cols", align_bytes=64)
+        query_raw = sb.tile([P, PACK, Q], F32, name="query_raw", tag="query_raw", align_bytes=64)
+        gout_raw = sb.tile([P, PACK, Q], F32, name="gout_raw", tag="gout_raw", align_bytes=64)
+        small_rows = sb.tile([P, P], F32, name="small_rows")
         ident = sb.tile([P, P], F32, name="ident")
-        warm = sb.tile([P, 1], F32, name="warm")
 
-        nc.vector.memset(ks[:].bitcast(I32), 0)
-        nc.vector.memset(age_win[:], 0.0)
-        nc.vector.memset(vs[:].bitcast(I32), 0)
+        nc.gpsimd.memset(small_rows[:], 0.0)
+        nc.vector.memset(keys_s[:].bitcast(I32), 0)
+        nc.vector.memset(vals_s[:].bitcast(I32), 0)
         make_identity(nc, ident[:])
-        nc.scalar.activation(warm[:], ident[:, 0:1], ACT.Exp)
 
         def load_scales(dst, src):
             for b in range(4):
                 nc.sync.dma_start(dst[32 * b:32 * b + 4, :].bitcast(I32), src[0, 4 * b:4 * b + 4, :].bitcast(I32))
 
-        def load_column(dst, src):
-            with nc.allow_non_contiguous_dma(reason="one value a partition"):
-                nc.sync.dma_start(dst[:], src)
-
-        nc.sync.dma_start(offsets[:], offs)
-        nc.sync.dma_start(kw[:].bitcast(I32), keys_words[0].bitcast(I32))
-        nc.sync.dma_start(q_raw[:], query.rearrange("(p j) w -> p j w", j=PACK))
-        load_scales(ks, keys_scales)
-        nc.sync.dma_start(vw[:].bitcast(I32), vals_words[0].bitcast(I32))
-        nc.sync.dma_start(g_raw[:], gout.rearrange("(p j) w -> p j w", j=PACK))
-        nc.sync.dma_start(age_win[0:1, :], age[0:1, :])
-        load_column(rate_sb, rate)
-        nc.sync.dma_start(kr0[0][:], keyrows[0:P, 0:T // 2])
-        load_scales(vs, vals_scales)
-        nc.sync.dma_start(kr0[1][:], keyrows[0:P, T // 2:T])
-        load_column(size_c, size.rearrange("o (p j) -> p (o j)", j=PACK))
-        load_column(reserve_sb, reserve)
-        load_column(fs_c, fs.rearrange("o (p j) -> p (o j)", j=PACK))
-        for j in range(1, 4):
-            nc.sync.dma_start(kr[j - 1][:], keyrows[j * P:(j + 1) * P, :])
-        nc.sync.dma_start(res_sb[:], res)
+        def load_keyrows(block, tag):
+            window = sb.tile([P, T], F32, name="keyrows%d" % block, tag=tag, align_bytes=64)
+            nc.sync.dma_start(window[:], keyrows[block * P:(block + 1) * P, :])
+            return window
 
         def quantize(name, grouped):
             codes = sb.tile([P, P], U32, name=name + "_codes", align_bytes=64)
             scales = sb.tile([P, P], U8, name=name + "_scales", align_bytes=64)
-            nc.vector.quantize_mx(out=codes[:].bitcast(FP8X4), scales=scales[:], in_=grouped[:])
+            nc.vector.quantize_mx(out=codes[:].bitcast(FP8X4), scales=scales[:], in_=grouped)
             return codes, scales
 
-        def interleave(name, raw):
-            grouped = sb.tile([P, Q * PACK], BF16, name=name + "_grp", align_bytes=64)
-            nc.scalar.copy(grouped[:].rearrange("p (w j) -> p w j", j=PACK), raw[:].rearrange("p j w -> p w j"))
-            return grouped
+        def interleave(grouped, raw):
+            nc.scalar.copy(grouped.rearrange("p (w j) -> p w j", j=PACK), raw[:].rearrange("p j w -> p w j"))
 
-        def gather(name, window, dtype):
-            got = sb.tile([P, I], dtype, name=name, align_bytes=64)
+        def gather(name, window, dtype, tag):
+            got = sb.tile([P, I], dtype, name=name, tag=tag, align_bytes=64)
             nc.vector.tensor_copy(got[:], window[:].indirect(offsets[:]))
             return got
 
-        def turn_pairs(name, rows):
-            words = rows[:].bitcast(F32)
+        def turn_pairs(by_slot, grouped):
+            words = by_slot[:].bitcast(F32)
             bank = turn.tile([P, 2, P], F32, name="turn")
-            for u in range(2):
-                nc.tensor.transpose(bank[:, u, :], words[:, u:2 * P:2], ident[:])
-            grouped = sb.tile([P, P * PACK], BF16, name=name + "_grp", align_bytes=64)
-            nc.scalar.copy(grouped[:].bitcast(F32).rearrange("p (r u) -> p r u", u=2), bank[:].rearrange("p u r -> p r u"))
-            return grouped
+            for h in range(2):
+                nc.tensor.transpose(bank[:, h, :], words[:, h:2 * P:2], ident[:])
+            nc.scalar.copy(grouped.bitcast(F32).rearrange("p (x h) -> p x h", h=2), bank[:].rearrange("p h x -> p x h"))
 
-        def spread(name, cols):
-            bank = ps.tile([P, PACK, P], F32, name=name)
+        def spread(bank, cols):
             for j in range(PACK):
                 nc.tensor.transpose(bank[:, j, :], cols[:, j:j + 1].to_broadcast([P, P]), ident[:])
-            return bank
 
-        kw_g = gather("kw_g", kw, U16)
-        q_grp = interleave("q", q_raw)
-        ks_g = gather("ks_g", ks, U8)
-        q_codes, q_scales = quantize("q", q_grp)
-        a_ps = ps.tile([P, I], F32, name="bank_a")
-        nc.tensor.matmul_mx(out=a_ps[:], lhsT=q_codes[:].bitcast(FP8X4), lhsT_scale=q_scales[:],
-                            rhs=kw_g[:].bitcast(FP4X4), rhs_scale=ks_g[:], start=True, stop=True)
-        age_g = gather("age_g", age_win, F32)
-        age_t = turn.tile([P, PACK, P], F32, name="turn")
-        for j in range(PACK):
-            nc.tensor.transpose(age_t[:, j, :], age_g[:, j * P:(j + 1) * P], ident[:])
-        age_c = sb.tile([P, PACK], F32, name="age_c")
-        nc.scalar.copy(age_c[:], age_t[:, :, 0])
-        age_bc = spread("age_bc", age_c)
-        fade = sb.tile([P, I], F32, name="fade")
-        nc.scalar.activation(fade[:], age_bc[:].rearrange("p j s -> p (j s)"), ACT.Copy, scale=rate_sb[:])
-        vw_g = gather("vw_g", vw, U16)
-        g_grp = interleave("go", g_raw)
-        vs_g = gather("vs_g", vs, U8)
-        go_codes, go_scales = quantize("go", g_grp)
-        c_ps = ps.tile([P, I], F32, name="bank_c")
-        nc.tensor.matmul_mx(out=c_ps[:], lhsT=go_codes[:].bitcast(FP8X4), lhsT_scale=go_scales[:],
-                            rhs=vw_g[:].bitcast(FP4X4), rhs_scale=vs_g[:], start=True, stop=True)
-        size_bc = spread("size_bc", size_c)
-        size_sb = sb.tile([P, I], F32, name="size_sb")
-        nc.scalar.copy(size_sb[:].rearrange("p (s j) -> p s j", j=PACK), size_bc[:].rearrange("p j s -> p s j"))
-        fs_bc = spread("fs_bc", fs_c)
+        nc.sync.dma_start(offsets[:], offs)
+        nc.sync.dma_start(age_cols[:], age[0:1, :].rearrange("o (p c) -> p (o c)", p=P))
+        nc.sync.dma_start(keys_w[:].bitcast(I32), keys_words[0].bitcast(I32))
+        nc.sync.dma_start(small_rows[SIZE_AT:FS_AT, :], size.rearrange("o (j p) -> (o j) p", p=P))
+        nc.sync.dma_start(small_rows[FS_AT:RATE_AT, :], fs.rearrange("o (j p) -> (o j) p", p=P))
+        nc.sync.dma_start(small_rows[RATE_AT:RESERVE_AT, :], rate.rearrange("p o -> o p"))
+        nc.sync.dma_start(small_rows[RESERVE_AT:SMALL_ROWS, :], reserve.rearrange("p o -> o p"))
+        nc.sync.dma_start(vals_w[:].bitcast(I32), vals_words[0].bitcast(I32))
+        nc.sync.dma_start(query_raw[:], query.rearrange("(p j) w -> p j w", j=PACK))
+        nc.sync.dma_start(gout_raw[:], gout.rearrange("(p j) w -> p j w", j=PACK))
+        load_scales(keys_s, keys_scales)
+        keyrows0 = load_keyrows(0, "keyrows0")
+        load_scales(vals_s, vals_scales)
 
-        s_sb = sb.tile([P, I], F32, name="s_sb")
-        nc.vector.tensor_tensor(s_sb[:], a_ps[:], fade[:], ALU.subtract)
-        p_sb = sb.tile([P, I], F32, name="p_sb")
-        z0 = sb.tile([P, 1], F32, name="z0")
-        nc.scalar.activation(p_sb[:], s_sb[:], ACT.Exp, accum_out=z0[:])
-        u_sb = sb.tile([P, I], F32, name="u_sb")
-        nc.vector.tensor_tensor(u_sb[:], c_ps[:], size_sb[:], ALU.mult)
+        early_grp = sb.tile([P, BLOCKS * I], BF16, name="early_grp", align_bytes=64)
+        last_grp = sb.tile([P, I], BF16, name="last_grp", align_bytes=64)
+
+        age_by_token = age_win[:].rearrange("n (p c) -> n p c", p=P)
+        for c0 in range(0, T // P, PACK):
+            bank = turn.tile([P, PACK, P], F32, name="turn")
+            spread(bank, age_cols[:, c0:c0 + PACK])
+            nc.scalar.activation(age_by_token[:, :, c0:c0 + PACK], bank[:].rearrange("n j p -> n p j"), ACT.Copy)
+
+        keys_wg = gather("keys_wg", keys_w, U16, "keys_wg")
+        keyrows1 = load_keyrows(1, "keys_w")
+        vals_wg = gather("vals_wg", vals_w, U16, "vals_wg")
+        keyrows2 = load_keyrows(2, "vals_w")
+        cast_grp = sb.tile([P, 2 * Q * PACK], BF16, name="cast_grp", tag="age_cols", align_bytes=64)
+        query_grp, gout_grp = cast_grp[:, :Q * PACK], cast_grp[:, Q * PACK:]
+        interleave(query_grp, query_raw)
+        interleave(gout_grp, gout_raw)
+        small_t = held.tile([P, P], F32, name="bank_u")
+        nc.tensor.transpose(small_t[:], small_rows[:], ident[:])
+        small = sb.tile([P, SMALL_ROWS], F32, name="small")
+        nc.scalar.copy(small[:], small_t[:, 0:SMALL_ROWS])
+        keyrows3 = load_keyrows(LAST, "gout_raw")
+
+        keys_sg = gather("keys_sg", keys_s, U8, "keys_sg")
+        query_codes, query_scales = quantize("query", query_grp)
+        a_ps = held.tile([P, I], F32, name="bank_a")
+        nc.tensor.matmul_mx(out=a_ps[:], lhsT=query_codes[:].bitcast(FP8X4), lhsT_scale=query_scales[:],
+                            rhs=keys_wg[:].bitcast(FP4X4), rhs_scale=keys_sg[:], start=True, stop=True)
+        age_g = gather("age_g", age_win, F32, "query_raw")
+        gout_codes, gout_scales = quantize("gout", gout_grp)
+        res_sb = sb.tile([P, D], F32, name="res_sb", tag="age_cols", align_bytes=64)
+        nc.sync.dma_start(res_sb[:], res)
+        neg_score = sb.tile([P, I], F32, name="neg_score", tag="neg_score", align_bytes=64)
+        nc.vector.scalar_tensor_tensor(neg_score[:], age_g[:], small[:, RATE_AT:RATE_AT + 1], a_ps[:],
+                                       ALU.mult, ALU.subtract)
+
+        vals_sg = gather("vals_sg", vals_s, U8, "keys_wg")
+        c_ps = held.tile([P, BLOCKS, P], F32, name="bank_c")
+        for j in range(BLOCKS):
+            nc.tensor.matmul_mx(out=c_ps[:, j, :], lhsT=vals_wg[:, j * P:(j + 1) * P].bitcast(FP4X4),
+                                lhsT_scale=vals_sg[:, j * P:(j + 1) * P], rhs=gout_codes[:].bitcast(FP8X4),
+                                rhs_scale=gout_scales[:], start=True, stop=True)
+
+        keyrows0_bf = sb.tile([P, T], BF16, name="keyrows0_bf", align_bytes=64)
+        for lo in range(0, T, BANK):
+            nc.scalar.activation(keyrows0_bf[:, lo:lo + BANK], keyrows0[:, lo:lo + BANK], ACT.Copy)
+
+        p_sb = sb.tile([P, I], F32, name="p_sb", tag="keyrows0", align_bytes=64)
+        p_sum = sb.tile([P, 1], F32, name="p_sum", tag="p_sum", align_bytes=64)
+        nc.scalar.activation(p_sb[:], neg_score[:], ACT.Exp, scale=-1.0, accum_out=p_sum[:])
         z = sb.tile([P, 1], F32, name="z")
-        nc.vector.tensor_tensor(z[:], z0[:], reserve_sb[:], ALU.add)
-        rz = sb.tile([P, 1], F32, name="rz")
-        nc.vector.reciprocal(rz[:], z[:])
-        t_sb = sb.tile([P, I], F32, name="t_sb")
-        r1 = sb.tile([P, 1], F32, name="r1")
-        nc.vector.scalar_tensor_tensor(t_sb[:], u_sb[:], rz[:], p_sb[:], ALU.mult, ALU.mult, accum_out=r1[:])
-        w_sb = sb.tile([P, I], F32, name="w_sb")
-        nc.vector.scalar_tensor_tensor(w_sb[:].rearrange("p (s j) -> p s j", j=PACK),
-                                       p_sb[:].rearrange("p (s j) -> p s j", j=PACK), rz[:],
-                                       fs_bc[:].rearrange("p j s -> p s j"), ALU.mult, ALU.mult)
+        nc.scalar.activation(z[:], p_sum[:], ACT.Identity, bias=small[:, RESERVE_AT:RESERVE_AT + 1])
+        fs_ps = held.tile([P, PACK, P], F32, name="bank_fs")
+        spread(fs_ps, small[:, FS_AT:RATE_AT])
+        u_t = [sb.tile([P, 2, P], F32, name="u_t%d" % h, tag=tag, align_bytes=64)
+               for h, tag in enumerate(("neg_score", "u_t1"))]
+        for j in range(BLOCKS):
+            nc.scalar.activation(u_t[j // 2][:, j % 2, :], c_ps[:, j, :], ACT.Copy,
+                                 scale=small[:, SIZE_AT + j:SIZE_AT + j + 1])
+        inv_z = sb.tile([P, 1], F32, name="inv_z")
+        nc.vector.reciprocal(inv_z[:], z[:])
+        kt1 = gather("kt1", keyrows1, BF16, "p_sum")
+        turn_pairs(kt1, early_grp[:, I:2 * I])
+        u_ps = held.tile([P, I], F32, name="bank_u")
+        for j in range(BLOCKS):
+            nc.tensor.transpose(u_ps[:, j * P:(j + 1) * P], u_t[j // 2][:, j % 2, :], ident[:])
+        weight = sb.tile([P, I], F32, name="weight")
+        nc.vector.scalar_tensor_tensor(weight[:], p_sb[:], inv_z[:], fs_ps[:].rearrange("p j s -> p (j s)"),
+                                       ALU.mult, ALU.mult)
+        kt0 = sb.tile([P, I], BF16, name="kt0", tag="neg_score", align_bytes=64)
+        nc.scalar.activation(kt0[:], keyrows0_bf[:].indirect(offsets[:]), ACT.Copy)
+        turn_pairs(kt0, early_grp[:, 0:I])
+        r_terms = sb.tile([P, I], F32, name="r_terms")
+        r = sb.tile([P, 1], F32, name="r")
+        nc.vector.scalar_tensor_tensor(r_terms[:], u_ps[:], inv_z[:], p_sb[:], ALU.mult, ALU.mult, accum_out=r[:])
         gs = sb.tile([P, I], BF16, name="gs", align_bytes=64)
-        nc.vector.scalar_tensor_tensor(gs[:], u_sb[:], r1[:], w_sb[:], ALU.subtract, ALU.mult)
-        gs_codes, gs_scales = quantize("gs", turn_pairs("gs", gs))
+        nc.vector.scalar_tensor_tensor(gs[:], u_ps[:], r[:], weight[:], ALU.subtract, ALU.mult)
+        turn_pairs(gs, early_grp[:, LAST * I:])
+        kt2 = gather("kt2", keyrows2, BF16, "u_t1")
+        turn_pairs(kt2, early_grp[:, 2 * I:3 * I])
+        kt3 = gather("kt3", keyrows3, BF16, "keyrows0")
+        turn_pairs(kt3, last_grp[:])
 
-        kr0_bf = sb.tile([P, T], BF16, name="kr0_bf", align_bytes=64)
-        for c in range(4):
-            nc.scalar.activation(kr0_bf[:, c * 512:(c + 1) * 512], kr0[c // 2][:, (c % 2) * 512:(c % 2 + 1) * 512], ACT.Copy)
-        kt0 = sb.tile([P, I], BF16, name="kt0", align_bytes=64)
-        nc.scalar.activation(kt0[:], kr0_bf[:].indirect(offsets[:]), ACT.Copy)
-        o_ps = [ps.tile([P, 3 * P], F32, name="bank_a"), ps.tile([P, P], F32, name="bank_c")]
-        for j in range(4):
-            rows = kt0 if j == 0 else gather("kt%d" % j, kr[j - 1], BF16)
-            codes, scales = quantize("kt%d" % j, turn_pairs("kt%d" % j, rows))
-            dst = o_ps[0][:, j * P:(j + 1) * P] if j < 3 else o_ps[1][:]
-            nc.tensor.matmul_mx(out=dst, lhsT=gs_codes[:].bitcast(FP8X4), lhsT_scale=gs_scales[:],
-                                rhs=codes[:].bitcast(FP8X4), rhs_scale=scales[:], start=True, stop=True)
-        for k, (lo, hi) in enumerate(((0, 3 * P), (3 * P, D))):
-            y = sb.tile([P, hi - lo], F32, name="y%d" % k)
-            nc.vector.tensor_tensor(y[:], o_ps[k][:], res_sb[:, lo:hi], ALU.add)
+        early_codes = sb.tile([P, BLOCKS * P], U32, name="early_codes", tag="gout_raw", align_bytes=64)
+        early_scales = sb.tile([P, BLOCKS * P], U8, name="early_scales", align_bytes=64)
+        nc.vector.quantize_mx(out=early_codes[:].bitcast(FP8X4), scales=early_scales[:], in_=early_grp[:])
+
+        early_ps = held.tile([P, LAST * P], F32, name="bank_a")
+        last_ps = held.tile([P, P], F32, name="bank_c")
+
+        def product(dst, codes, scales):
+            nc.tensor.matmul_mx(out=dst, lhsT=early_codes[:, LAST * P:].bitcast(FP8X4),
+                                lhsT_scale=early_scales[:, LAST * P:], rhs=codes.bitcast(FP8X4), rhs_scale=scales,
+                                start=True, stop=True)
+
+        def finish(name, bank, lo, hi):
+            y = sb.tile([P, hi - lo], F32, name=name)
+            nc.vector.tensor_tensor(y[:], bank[:], res_sb[:, lo:hi], ALU.add)
             nc.sync.dma_start(out[:, lo:hi], y[:])
+
+        for lo, hi in ((0, 2 * P), (2 * P, LAST * P)):
+            product(early_ps[:, lo:hi], early_codes[:, lo:hi], early_scales[:, lo:hi])
+        last_codes, last_scales = quantize("last", last_grp[:])
+        product(last_ps[:], last_codes[:], last_scales[:])
+        finish("y_early", early_ps, 0, LAST * P)
+        finish("y_last", last_ps, LAST * P, D)

from contextlib import ExitStack

import concourse.mybir as mybir
from concourse.masks import make_identity

D, E, T, I, Q = 512, 512, 2048, 512, 128
FLOPS = 2 * Q * I * (D + E + D)

P = 128
PACK = 4
BANK = 512
BLOCKS = D // P
LAST = BLOCKS - 1
TURN_BANKS = 4
SIZE_AT, FS_AT, RATE_AT, RESERVE_AT, SMALL_ROWS = 0, 4, 8, 9, 10

F32 = mybir.dt.float32
BF16 = mybir.dt.bfloat16
I32 = mybir.dt.int32
U32 = mybir.dt.uint32
U16 = mybir.dt.uint16
U8 = mybir.dt.uint8
FP8X4 = mybir.dt.float8_e4m3fn_x4
FP4X4 = mybir.dt.float4_e2m1fn_x4
ALU = mybir.AluOpType
ACT = mybir.ActivationFunctionType


def tile_attend_bfadereserve_q_kernel(tc, query, keys_words, keys_scales, age, rate, reserve, gout,
                                       vals_words, vals_scales, size, fs, keyrows, res, offs, out):
    nc = tc.nc
    with ExitStack() as ctx:
        sb = ctx.enter_context(tc.tile_pool(name="sb", bufs=1))
        held = ctx.enter_context(tc.psum_pool(name="held", bufs=1))
        turn = ctx.enter_context(tc.psum_pool(name="turn", bufs=TURN_BANKS))

        offsets = sb.tile([P, I // 16], U16, name="offsets")
        keys_w = sb.tile([P, T], U16, name="keys_w", tag="keys_w", align_bytes=64)
        vals_w = sb.tile([P, T], U16, name="vals_w", tag="vals_w", align_bytes=64)
        keys_s = sb.tile([P, T], U8, name="keys_s", align_bytes=64)
        vals_s = sb.tile([P, T], U8, name="vals_s", align_bytes=64)
        age_win = sb.tile([P, T], F32, name="age_win", align_bytes=64)
        age_cols = sb.tile([P, T // P], F32, name="age_cols", tag="age_cols", align_bytes=64)
        query_raw = sb.tile([P, PACK, Q], F32, name="query_raw", tag="query_raw", align_bytes=64)
        gout_raw = sb.tile([P, PACK, Q], F32, name="gout_raw", tag="gout_raw", align_bytes=64)
        small_rows = sb.tile([P, P], F32, name="small_rows")
        ident = sb.tile([P, P], F32, name="ident")

        nc.gpsimd.memset(small_rows[:], 0.0)
        nc.vector.memset(keys_s[:].bitcast(I32), 0)
        nc.vector.memset(vals_s[:].bitcast(I32), 0)
        make_identity(nc, ident[:])

        def load_scales(dst, src):
            for b in range(4):
                nc.sync.dma_start(dst[32 * b:32 * b + 4, :].bitcast(I32), src[0, 4 * b:4 * b + 4, :].bitcast(I32))

        def load_keyrows(block, tag):
            window = sb.tile([P, T], F32, name="keyrows%d" % block, tag=tag, align_bytes=64)
            nc.sync.dma_start(window[:], keyrows[block * P:(block + 1) * P, :])
            return window

        def quantize(name, grouped):
            codes = sb.tile([P, P], U32, name=name + "_codes", align_bytes=64)
            scales = sb.tile([P, P], U8, name=name + "_scales", align_bytes=64)
            nc.vector.quantize_mx(out=codes[:].bitcast(FP8X4), scales=scales[:], in_=grouped)
            return codes, scales

        def interleave(grouped, raw):
            nc.scalar.copy(grouped.rearrange("p (w j) -> p w j", j=PACK), raw[:].rearrange("p j w -> p w j"))

        def gather(name, window, dtype, tag):
            got = sb.tile([P, I], dtype, name=name, tag=tag, align_bytes=64)
            nc.vector.tensor_copy(got[:], window[:].indirect(offsets[:]))
            return got

        def turn_pairs(by_slot, grouped):
            words = by_slot[:].bitcast(F32)
            bank = turn.tile([P, 2, P], F32, name="turn")
            for h in range(2):
                nc.tensor.transpose(bank[:, h, :], words[:, h:2 * P:2], ident[:])
            nc.scalar.copy(grouped.bitcast(F32).rearrange("p (x h) -> p x h", h=2), bank[:].rearrange("p h x -> p x h"))

        def spread(bank, cols):
            for j in range(PACK):
                nc.tensor.transpose(bank[:, j, :], cols[:, j:j + 1].to_broadcast([P, P]), ident[:])

        nc.sync.dma_start(offsets[:], offs)
        nc.sync.dma_start(age_cols[:], age[0:1, :].rearrange("o (p c) -> p (o c)", p=P))
        nc.sync.dma_start(keys_w[:].bitcast(I32), keys_words[0].bitcast(I32))
        nc.sync.dma_start(small_rows[SIZE_AT:FS_AT, :], size.rearrange("o (j p) -> (o j) p", p=P))
        nc.sync.dma_start(small_rows[FS_AT:RATE_AT, :], fs.rearrange("o (j p) -> (o j) p", p=P))
        nc.sync.dma_start(small_rows[RATE_AT:RESERVE_AT, :], rate.rearrange("p o -> o p"))
        nc.sync.dma_start(small_rows[RESERVE_AT:SMALL_ROWS, :], reserve.rearrange("p o -> o p"))
        nc.sync.dma_start(vals_w[:].bitcast(I32), vals_words[0].bitcast(I32))
        nc.sync.dma_start(query_raw[:], query.rearrange("(p j) w -> p j w", j=PACK))
        nc.sync.dma_start(gout_raw[:], gout.rearrange("(p j) w -> p j w", j=PACK))
        load_scales(keys_s, keys_scales)
        keyrows0 = load_keyrows(0, "keyrows0")
        load_scales(vals_s, vals_scales)

        early_grp = sb.tile([P, BLOCKS * I], BF16, name="early_grp", align_bytes=64)
        last_grp = sb.tile([P, I], BF16, name="last_grp", align_bytes=64)

        age_by_token = age_win[:].rearrange("n (p c) -> n p c", p=P)
        for c0 in range(0, T // P, PACK):
            bank = turn.tile([P, PACK, P], F32, name="turn")
            spread(bank, age_cols[:, c0:c0 + PACK])
            nc.scalar.activation(age_by_token[:, :, c0:c0 + PACK], bank[:].rearrange("n j p -> n p j"), ACT.Copy)

        keys_wg = gather("keys_wg", keys_w, U16, "keys_wg")
        keyrows1 = load_keyrows(1, "keys_w")
        vals_wg = gather("vals_wg", vals_w, U16, "vals_wg")
        keyrows2 = load_keyrows(2, "vals_w")
        cast_grp = sb.tile([P, 2 * Q * PACK], BF16, name="cast_grp", tag="age_cols", align_bytes=64)
        query_grp, gout_grp = cast_grp[:, :Q * PACK], cast_grp[:, Q * PACK:]
        interleave(query_grp, query_raw)
        interleave(gout_grp, gout_raw)
        small_t = held.tile([P, P], F32, name="bank_u")
        nc.tensor.transpose(small_t[:], small_rows[:], ident[:])
        small = sb.tile([P, SMALL_ROWS], F32, name="small")
        nc.scalar.copy(small[:], small_t[:, 0:SMALL_ROWS])
        keyrows3 = load_keyrows(LAST, "gout_raw")

        keys_sg = gather("keys_sg", keys_s, U8, "keys_sg")
        query_codes, query_scales = quantize("query", query_grp)
        a_ps = held.tile([P, I], F32, name="bank_a")
        nc.tensor.matmul_mx(out=a_ps[:], lhsT=query_codes[:].bitcast(FP8X4), lhsT_scale=query_scales[:],
                            rhs=keys_wg[:].bitcast(FP4X4), rhs_scale=keys_sg[:], start=True, stop=True)
        age_g = gather("age_g", age_win, F32, "query_raw")
        gout_codes, gout_scales = quantize("gout", gout_grp)
        res_sb = sb.tile([P, D], F32, name="res_sb", tag="age_cols", align_bytes=64)
        nc.sync.dma_start(res_sb[:], res)
        neg_score = sb.tile([P, I], F32, name="neg_score", tag="neg_score", align_bytes=64)
        nc.vector.scalar_tensor_tensor(neg_score[:], age_g[:], small[:, RATE_AT:RATE_AT + 1], a_ps[:],
                                       ALU.mult, ALU.subtract)

        vals_sg = gather("vals_sg", vals_s, U8, "keys_wg")
        c_ps = held.tile([P, BLOCKS, P], F32, name="bank_c")
        for j in range(BLOCKS):
            nc.tensor.matmul_mx(out=c_ps[:, j, :], lhsT=vals_wg[:, j * P:(j + 1) * P].bitcast(FP4X4),
                                lhsT_scale=vals_sg[:, j * P:(j + 1) * P], rhs=gout_codes[:].bitcast(FP8X4),
                                rhs_scale=gout_scales[:], start=True, stop=True)

        keyrows0_bf = sb.tile([P, T], BF16, name="keyrows0_bf", align_bytes=64)
        for lo in range(0, T, BANK):
            nc.scalar.activation(keyrows0_bf[:, lo:lo + BANK], keyrows0[:, lo:lo + BANK], ACT.Copy)

        p_sb = sb.tile([P, I], F32, name="p_sb", tag="keyrows0", align_bytes=64)
        p_sum = sb.tile([P, 1], F32, name="p_sum", tag="p_sum", align_bytes=64)
        nc.scalar.activation(p_sb[:], neg_score[:], ACT.Exp, scale=-1.0, accum_out=p_sum[:])
        z = sb.tile([P, 1], F32, name="z")
        nc.scalar.activation(z[:], p_sum[:], ACT.Identity, bias=small[:, RESERVE_AT:RESERVE_AT + 1])
        fs_ps = held.tile([P, PACK, P], F32, name="bank_fs")
        spread(fs_ps, small[:, FS_AT:RATE_AT])
        u_t = [sb.tile([P, 2, P], F32, name="u_t%d" % h, tag=tag, align_bytes=64)
               for h, tag in enumerate(("neg_score", "u_t1"))]
        for j in range(BLOCKS):
            nc.scalar.activation(u_t[j // 2][:, j % 2, :], c_ps[:, j, :], ACT.Copy,
                                 scale=small[:, SIZE_AT + j:SIZE_AT + j + 1])
        inv_z = sb.tile([P, 1], F32, name="inv_z")
        nc.vector.reciprocal(inv_z[:], z[:])
        kt1 = gather("kt1", keyrows1, BF16, "p_sum")
        turn_pairs(kt1, early_grp[:, I:2 * I])
        u_ps = held.tile([P, I], F32, name="bank_u")
        for j in range(BLOCKS):
            nc.tensor.transpose(u_ps[:, j * P:(j + 1) * P], u_t[j // 2][:, j % 2, :], ident[:])
        weight = sb.tile([P, I], F32, name="weight")
        nc.vector.scalar_tensor_tensor(weight[:], p_sb[:], inv_z[:], fs_ps[:].rearrange("p j s -> p (j s)"),
                                       ALU.mult, ALU.mult)
        kt0 = sb.tile([P, I], BF16, name="kt0", tag="neg_score", align_bytes=64)
        nc.scalar.activation(kt0[:], keyrows0_bf[:].indirect(offsets[:]), ACT.Copy)
        turn_pairs(kt0, early_grp[:, 0:I])
        r_terms = sb.tile([P, I], F32, name="r_terms")
        r = sb.tile([P, 1], F32, name="r")
        nc.vector.scalar_tensor_tensor(r_terms[:], u_ps[:], inv_z[:], p_sb[:], ALU.mult, ALU.mult, accum_out=r[:])
        gs = sb.tile([P, I], BF16, name="gs", align_bytes=64)
        nc.vector.scalar_tensor_tensor(gs[:], u_ps[:], r[:], weight[:], ALU.subtract, ALU.mult)
        turn_pairs(gs, early_grp[:, LAST * I:])
        kt2 = gather("kt2", keyrows2, BF16, "u_t1")
        turn_pairs(kt2, early_grp[:, 2 * I:3 * I])
        kt3 = gather("kt3", keyrows3, BF16, "keyrows0")
        turn_pairs(kt3, last_grp[:])

        early_codes = sb.tile([P, BLOCKS * P], U32, name="early_codes", tag="gout_raw", align_bytes=64)
        early_scales = sb.tile([P, BLOCKS * P], U8, name="early_scales", align_bytes=64)
        nc.vector.quantize_mx(out=early_codes[:].bitcast(FP8X4), scales=early_scales[:], in_=early_grp[:])

        early_ps = held.tile([P, LAST * P], F32, name="bank_a")
        last_ps = held.tile([P, P], F32, name="bank_c")

        def product(dst, codes, scales):
            nc.tensor.matmul_mx(out=dst, lhsT=early_codes[:, LAST * P:].bitcast(FP8X4),
                                lhsT_scale=early_scales[:, LAST * P:], rhs=codes.bitcast(FP8X4), rhs_scale=scales,
                                start=True, stop=True)

        def finish(name, bank, lo, hi):
            y = sb.tile([P, hi - lo], F32, name=name)
            nc.vector.tensor_tensor(y[:], bank[:], res_sb[:, lo:hi], ALU.add)
            nc.sync.dma_start(out[:, lo:hi], y[:])

        for lo, hi in ((0, 2 * P), (2 * P, LAST * P)):
            product(early_ps[:, lo:hi], early_codes[:, lo:hi], early_scales[:, lo:hi])
        last_codes, last_scales = quantize("last", last_grp[:])
        product(last_ps[:], last_codes[:], last_scales[:])
        finish("y_early", early_ps, 0, LAST * P)
        finish("y_last", last_ps, LAST * P, D)
